import numpy as np
import ml_dtypes


def mxq(x, axis, fmt="e4m3"):
    dtype, down = {"e4m3": (ml_dtypes.float8_e4m3fn, 7), "e5m2": (ml_dtypes.float8_e5m2, 14)}[fmt]
    v = np.moveaxis(np.asarray(x, np.float32).astype(ml_dtypes.bfloat16).astype(np.float64), axis, -1)
    blocks = v.reshape(v.shape[:-1] + (-1, 32))
    amax = np.abs(blocks).max(-1, keepdims=True)
    byte = np.maximum(np.where(amax > 0, np.frexp(amax)[1] - 1 + 127, 0) - down, 1)
    scale = np.exp2(byte - 127.0)
    codes = (blocks / scale).astype(np.float32).astype(dtype).astype(np.float64)
    return np.moveaxis((codes * scale).reshape(v.shape), -1, axis)


WIDE = False


def mx_kscale(k):
    if not WIDE:
        return np.ones(k)
    levels = np.array([10, -10, 5, -5, 0])
    if k % 512:
        return np.exp2(np.random.permutation(np.resize(levels, k // 32))).repeat(32)
    a = np.empty((k // 512, 16))
    for p in range(k // 512):
        a[p, :8] = np.random.permutation(np.resize(levels, 8))
        for g in range(8):
            far = levels[np.abs(levels - a[p, g]) >= 10]
            a[p, g + 8] = far[np.random.randint(len(far))]
    return np.exp2(a.ravel()).repeat(32)


def f64(x):
    return np.asarray(x).astype(np.float64)


def striped(idx):
    return np.tile(idx.reshape(-1, 16).T, (8, 1)).astype(np.uint16)


def unstriped(offs):
    return offs[:16].T.reshape(-1).astype(np.int64)


def striped8(idx):
    return np.concatenate([x.reshape(-1, 16).T for x in idx]).astype(np.uint16)


def runs(offs, k):
    lists = np.stack([offs[16 * r : 16 * r + 16].T.reshape(-1) for r in range(8)]).astype(np.int64)
    return lists[np.arange(k) % 512 // 64]


def pack_weight(w):
    k, n = w.shape
    w = f64(np.asarray(w, np.float32).astype(ml_dtypes.bfloat16)).reshape(k // 32, 32, n)
    amax = np.abs(w).max(1)
    byte = np.clip(np.where(amax > 0, np.frexp(amax)[1] - 1 + 127 - 7, 1), 1, 254)
    scaled = (w * np.exp2(127.0 - byte)[:, None, :]).reshape(k, n).astype(np.float32)
    words = np.ascontiguousarray(scaled.reshape(k // 512, 128, 4, n).transpose(0, 1, 3, 2)).astype(ml_dtypes.float8_e4m3fn).view(np.uint8)
    return words, np.ascontiguousarray(byte.astype(np.uint8).reshape(k // 512, 16, n))


def unpack_weight(words, scales):
    g, p, n, _ = words.shape
    vals = np.ascontiguousarray(words).view(ml_dtypes.float8_e4m3fn).astype(np.float64) * np.repeat(np.exp2(scales.astype(np.float64) - 127.0), 8, axis=1)[..., None]
    return vals.transpose(0, 1, 3, 2).reshape(g * 512, n)


E2M1 = np.array([0.0, 0.5, 1.0, 1.5, 2.0, 3.0, 4.0, 6.0, -0.0, -0.5, -1.0, -1.5, -2.0, -3.0, -4.0, -6.0])


def pack_fp4(w):
    k, n = w.shape
    w = f64(np.asarray(w, np.float32).astype(ml_dtypes.bfloat16)).reshape(k // 32, 32, n)
    amax = np.abs(w).max(1)
    mant, ex = np.frexp(amax / 6.0)
    byte = np.clip(np.where(amax > 0, np.where(mant > 0.5, ex, ex - 1) + 127, 1), 1, 254)
    scaled = (w * np.exp2(127.0 - byte)[:, None, :]).reshape(k, n).astype(np.float32)
    c = np.ascontiguousarray(scaled.reshape(k // 512, 128, 4, n).transpose(0, 1, 3, 2)).astype(ml_dtypes.float4_e2m1fn).view(np.uint8) & 0xF
    words = (c[..., 0::2] | (c[..., 1::2] << 4)).reshape(k // 512, 128, 2 * n)
    return np.ascontiguousarray(words), np.ascontiguousarray(byte.astype(np.uint8).reshape(k // 512, 16, n))


def unpack_fp4(words, scales):
    g, _, n = scales.shape
    words = np.ascontiguousarray(words).reshape(g, 128, n, 2)
    nib = np.empty((g, 128, n, 4), np.uint8)
    nib[..., 0::2] = words & 0xF
    nib[..., 1::2] = words >> 4
    vals = E2M1[nib] * np.repeat(np.exp2(scales.astype(np.float64) - 127.0), 8, axis=1)[..., None]
    return vals.transpose(0, 1, 3, 2).reshape(g * 512, n)


def planes(y):
    n, m = y.shape
    v = y.astype(np.float32).astype(ml_dtypes.bfloat16).astype(np.float64).reshape(n // 32, 32, m)
    top = np.abs(v).max(1)
    byte = np.clip(np.where(top > 0, np.frexp(top)[1] - 1 + 127 - 7, 1), 1, 254)
    codes = (v * np.exp2(127.0 - byte)[:, None, :]).reshape(n, m).astype(np.float32).astype(ml_dtypes.float8_e4m3fn).view(np.uint8)
    words = codes.reshape(n // 512, 128, 4, m).transpose(0, 1, 3, 2)
    return np.ascontiguousarray(words), np.ascontiguousarray(byte.astype(np.uint8).reshape(n // 512, 16, m))


K, T, S, N, G, H = 512, 1024, 256, 512, 2048, 512


def setup_inputs():
    n = np.random.standard_normal
    s = mx_kscale(K)[:, None]
    u = mx_kscale(K)
    packed_xT = pack_weight(n((K, T)) * s)
    packed_dT = pack_weight(n((K, G)) / s)
    packed_w1 = pack_fp4(n((H, N)) / np.sqrt(H) / u[:, None])
    return {
        "x_words": packed_xT[0],
        "x_scales": packed_xT[1],
        "d_words": packed_dT[0],
        "d_scales": packed_dT[1],
        "gn": (np.random.uniform(0.5, 1.5, (H, 1)) * u[:, None]).astype(np.float32),
        "w1_words": packed_w1[0],
        "w1_scales": packed_w1[1],
        "offs": striped(np.random.permutation(T)[:S]),
        "k1": striped8(np.random.randint(0, G, (8, H))),
        "two": striped(np.random.permutation(T)[:S]),
        "k2": striped8(np.random.randint(0, G, (8, H))),
        "n1": striped8(np.stack([np.random.permutation(S) for _ in range(8)])),
        "n2": striped8(np.stack([np.random.permutation(S) for _ in range(8)])),
        "n3": striped8(np.stack([np.random.permutation(S) for _ in range(8)])),
        "n4": striped8(np.stack([np.random.permutation(S) for _ in range(8)])),
        "n5": striped8(np.stack([np.random.permutation(S) for _ in range(8)])),
        "n6": striped8(np.stack([np.random.permutation(S) for _ in range(8)])),
    }


def reference(x_words, x_scales, d_words, d_scales, gn, w1_words, w1_scales, offs, k1, two, k2, n1, n2, n3, n4, n5, n6):
    d_k1 = unpack_weight(d_words, d_scales)[np.arange(K)[:, None], runs(k1, K)]
    xq = unpack_weight(x_words, x_scales)[:, unstriped(offs)]
    a = 0.0625 * (d_k1.T @ xq)
    d_k2 = unpack_weight(d_words, d_scales)[np.arange(K)[:, None], runs(k2, K)]
    x_two = unpack_weight(x_words, x_scales)[:, unstriped(two)]
    b = 0.0625 * (d_k2.T @ x_two)
    z = f64(gn) * (a * (np.tanh(b[np.arange(H)[:, None], runs(n1, H)] - (b[np.arange(H)[:, None], runs(n2, H)]))))
    h = unpack_fp4(w1_words, w1_scales).T @ mxq(z, 0, "e4m3")
    out_0 = 0.75 * ((h[np.arange(N)[:, None], runs(n3, N)]) * (h[np.arange(N)[:, None], runs(n4, N)]) - ((h[np.arange(N)[:, None], runs(n5, N)]) * (h[np.arange(N)[:, None], runs(n6, N)])))
    return (out_0,) + planes(out_0)

@@ -1,0 +1,214 @@
+from contextlib import ExitStack
+
+import concourse.mybir as mybir
+
+K, T, S, N, G, H = 512, 1024, 256, 512, 2048, 512
+FLOPS = 3 * 2 * 512 * 512 * 256
+
+F32 = mybir.dt.float32
+BF16 = mybir.dt.bfloat16
+I32 = mybir.dt.int32
+U32 = mybir.dt.uint32
+U16 = mybir.dt.uint16
+U8 = mybir.dt.uint8
+FP8X4 = mybir.dt.float8_e4m3fn_x4
+FP4X4 = mybir.dt.float4_e2m1fn_x4
+ACT = mybir.ActivationFunctionType
+ALU = mybir.AluOpType
+
+P = 128
+PACK = 4
+HALF = S // 2
+
+
+def tile_picked_twpqjointbdet_none_po_kernel(
+    tc, x_words, x_scales, d_words, d_scales, gn, w1_words, w1_scales,
+    offs, k1, two, k2, n1, n2, n3, n4, n5, n6, out_0, out_1, out_2,
+):
+    nc = tc.nc
+    with ExitStack() as ctx:
+        sb = ctx.enter_context(tc.tile_pool(name="sb", bufs=1))
+        picks = ctx.enter_context(tc.tile_pool(name="picks", bufs=1))
+        ps = ctx.enter_context(tc.psum_pool(name="ps", bufs=1))
+
+        def sbuf(name, shape, dtype):
+            return sb.tile(shape, dtype, name=name, align_bytes=64)
+
+        def load_list(name, src):
+            tile = sbuf(name, list(src.shape), U16)
+            nc.sync.dma_start(tile[:], src)
+            return tile
+
+        d_bytes = sbuf("d_bytes", [P, G], U8)
+        x_bytes = sbuf("x_bytes", [P, T], U8)
+
+        def load_scale_rows(tile, scales):
+            words = scales[0].bitcast(I32)
+            nc.sync.dma_start(tile[:].bitcast(I32), words.unsqueeze(1).to_broadcast([16, 8, words.shape[1]]))
+
+        def placed(name, shape, dtype, offset):
+            return picks.tile(shape, dtype, name=name, align_bytes=64, offset=offset)
+
+        k2_l = load_list("k2_l", k2)
+        load_scale_rows(d_bytes, d_scales)
+        two_l = load_list("two_l", two)
+        load_scale_rows(x_bytes, x_scales)
+        k1_l = load_list("k1_l", k1)
+        offs_l = load_list("offs_l", offs)
+        d_tab = sbuf("d_tab", [P, G], I32)
+        x_tab = sbuf("x_tab", [P, T], I32)
+        nc.sync.dma_start(x_tab[:], x_words[0].rearrange("p n r -> p (n r)").bitcast(I32))
+        nc.sync.dma_start(d_tab[:], d_words[0].rearrange("p n r -> p (n r)").bitcast(I32))
+
+        gain_raw = sbuf("gain_raw", [P, PACK], F32)
+        nc.gpsimd.dma_start(gain_raw[:], gn.rearrange("(p t) o -> p (t o)", t=PACK))
+        w_raw = sbuf("w_raw", [P, 2 * N], U8)
+        nc.gpsimd.dma_start(w_raw[:].bitcast(I32), w1_words[0].bitcast(I32))
+
+        gain = sbuf("gain", [P, PACK], F32)
+        nc.scalar.activation(gain[:], gain_raw[:], ACT.Copy, scale=0.0625)
+        w_codes = sbuf("w_codes", [P, 2 * N], U8)
+        nc.scalar.copy(
+            w_codes[:].bitcast(U16).rearrange("p (t m) -> p t m", t=PACK),
+            w_raw[:].bitcast(U16).rearrange("p (m t) -> p t m", t=PACK),
+        )
+
+        widths = [2 * S, 2 * S, 2 * S, S]
+        rows = [sbuf("rows%d" % t, [P, widths[t]], F32) for t in range(PACK)]
+        for t in range(PACK - 1):
+            nc.vector.memset(rows[t][:, S:], 0.0)
+
+        def deal_bytes(dst, src):
+            nc.vector.tensor_copy(dst.rearrange("p (t m) -> p t m", t=PACK), src.rearrange("p (m t) -> p t m", t=PACK))
+
+        def coded_scales(picked, plane, k_l, x_l):
+            nc.vector.tensor_copy(picked[:, :H], d_bytes[:].indirect(k_l[:]))
+            nc.vector.tensor_copy(picked[:, H:], x_bytes[:].indirect(x_l[:]))
+            deal_bytes(plane[:, :H], picked[:, :H])
+            nc.vector.tensor_copy(plane[:, H : H + S].bitcast(I32), picked[:, H:].bitcast(I32))
+
+        def seat_rows(plane):
+            for r in range(1, 4):
+                nc.sync.dma_start(plane[r:P:32, :].bitcast(I32), plane[8 * r : P : 32, :].bitcast(I32))
+
+        def coded_words(d_picked, d_dealt, x_picked, k_l, x_l):
+            nc.vector.tensor_copy(x_picked[:].bitcast(U32), x_tab[:].bitcast(U32).indirect(x_l[:]))
+            nc.vector.tensor_copy(d_picked[:].bitcast(U32), d_tab[:].bitcast(U32).indirect(k_l[:]))
+            nc.vector.tensor_copy(
+                d_dealt[:].rearrange("p (t c i) -> p c t i", t=PACK, i=4),
+                d_picked[:].rearrange("p (c i t) -> p c t i", t=PACK, i=4),
+            )
+
+        def coded_product(acc, t, d_dealt, x_picked, plane):
+            cols = slice(P * t, P * (t + 1))
+            nc.tensor.matmul_mx(
+                acc, lhsT=d_dealt[:, cols].bitcast(FP8X4), lhsT_scale=plane[:, cols],
+                rhs=x_picked[:].bitcast(FP8X4), rhs_scale=plane[:, H : H + S], start=True, stop=True,
+            )
+
+        plane_b = sbuf("plane_b", [P, H + S], U8)
+        coded_scales(placed("bytes_b", [P, H + S], U8, 8704), plane_b, k2_l, two_l)
+        seat_rows(plane_b)
+        w_bytes = placed("w_bytes", [P, N], U8, 8704)
+        nc.gpsimd.memset(w_bytes[:].bitcast(I32), 0)
+        for q in range(4):
+            nc.sync.dma_start(w_bytes[32 * q : 32 * q + 4, :].bitcast(I32), w1_scales[0, 4 * q : 4 * q + 4, :].bitcast(I32))
+        d_b = sbuf("d_b", [P, H], I32)
+        x_b = sbuf("x_b", [P, S], I32)
+        coded_words(placed("d_picked_b", [P, H], I32, 6016), d_b, x_b, k2_l, two_l)
+        b_acc = [ps.tile([P, S], F32, name="b_acc%d" % t, tag="bank%d" % t) for t in range(PACK)]
+        for t in range(PACK):
+            coded_product(b_acc[t][:], t, d_b, x_b, plane_b)
+
+        n_l = [load_list("n%d_l" % (i + 1), src) for i, src in enumerate((n1, n2, n3, n4, n5, n6))]
+        plane_a = placed("plane_a", [P, H + S], U8, 7872)
+        coded_scales(placed("bytes_a", [P, H + S], U8, 6080), plane_a, k1_l, offs_l)
+        seat_rows(plane_a)
+        d_a = sbuf("d_a", [P, H], I32)
+        x_a = placed("x_a", [P, S], I32, 6848)
+        coded_words(placed("d_picked_a", [P, H], I32, 4032), d_a, x_a, k1_l, offs_l)
+        w_plane = placed("w_plane", [P, N], U8, 6080)
+        deal_bytes(w_plane[:], w_bytes[:])
+        a_acc = [ps.tile([P, 2, S], F32, name="a_acc%d" % u) for u in range(2)]
+        for t in range(PACK):
+            coded_product(a_acc[t // 2][:, t % 2, :], t, d_a, x_a, plane_a)
+
+        def fetch(out, t, lst, c0, c1):
+            nc.scalar.activation(out, rows[t][:].indirect(lst[:, c0 // 16 : c1 // 16]), ACT.Copy)
+
+        pieces = [(0, 0, S), (1, 0, S), (2, 0, S), (3, 0, HALF), (3, HALF, S)]
+
+        b_at = [sbuf("b_at%d" % i, [P, PACK, S], F32) for i in range(2)]
+        diff = sbuf("diff", [P, PACK, S], F32)
+        th = placed("th", [P, PACK, S], F32, 0)
+        z = sbuf("z", [P, PACK, S], F32)
+        z_bf = sbuf("z_bf", [P, S, PACK], BF16)
+        z_codes = sbuf("z_codes", [P, S], I32)
+        z_plane = sbuf("z_plane", [P, S], U8)
+        h_first = ps.tile([P, PACK, HALF], F32, name="h_first")
+        h_lead = ps.tile([P, HALF], F32, name="h_lead")
+        h_rest = ps.tile([P, PACK - 1, HALF], F32, name="h_rest", tag="bank0")
+
+        def round_and_quantise(src, bf, codes, plane, c0, c1):
+            nc.vector.tensor_copy(
+                bf[:, c0:c1, :].rearrange("p (c i) t -> p c t i", i=4),
+                src[:, :, c0:c1].rearrange("p t (c i) -> p c t i", i=4),
+            )
+            nc.vector.quantize_mx(
+                out=codes[:, c0:c1].bitcast(FP8X4), scales=plane[:, c0:c1],
+                in_=bf[:, c0:c1, :].rearrange("p c t -> p (c t)"),
+            )
+
+        def dense(acc, t, c0, c1):
+            nc.tensor.matmul_mx(
+                acc, lhsT=w_codes[:, 2 * P * t : 2 * P * (t + 1)].bitcast(FP4X4), lhsT_scale=w_plane[:, P * t : P * (t + 1)],
+                rhs=z_codes[:, c0:c1].bitcast(FP8X4), rhs_scale=z_plane[:, c0:c1], start=True, stop=True,
+            )
+
+        for t, c0, c1 in pieces:
+            if c0 == 0:
+                nc.scalar.copy(rows[t][:, :S], b_acc[t][:])
+            fetch(b_at[0][:, t, c0:c1], t, n_l[0], c0, c1)
+            fetch(b_at[1][:, t, c0:c1], t, n_l[1], c0, c1)
+            nc.vector.tensor_tensor(diff[:, t, c0:c1], b_at[0][:, t, c0:c1], b_at[1][:, t, c0:c1], ALU.subtract)
+            nc.scalar.activation(th[:, t, c0:c1], diff[:, t, c0:c1], ACT.Tanh, scale=0.0625)
+            nc.vector.scalar_tensor_tensor(
+                z[:, t, c0:c1], a_acc[t // 2][:, t % 2, c0:c1], gain[:, t : t + 1], th[:, t, c0:c1], ALU.mult, ALU.mult
+            )
+            if t == PACK - 1:
+                round_and_quantise(z, z_bf, z_codes, z_plane, c0, c1)
+
+        for t in range(PACK):
+            dense(h_first[:, t, :], t, 0, HALF)
+        dense(h_lead[:], 0, HALF, S)
+        for t in range(1, PACK):
+            dense(h_rest[:, t - 1, :], t, HALF, S)
+        for t in range(PACK):
+            nc.scalar.copy(rows[t][:, :HALF], h_first[:, t, :])
+        nc.scalar.copy(rows[0][:, HALF:S], h_lead[:])
+        for t in range(1, PACK):
+            nc.vector.tensor_copy(rows[t][:, HALF:S], h_rest[:, t - 1, :])
+
+        h_at = [sbuf("h_at%d" % t, [P, 4, S], F32) for t in range(PACK)]
+        prod = [sbuf("prod%d" % t, [P, 2, S], F32) for t in range(PACK)]
+        y = sbuf("y", [P, PACK, S], F32)
+        y_bf = sbuf("y_bf", [P, S, PACK], BF16)
+        y_codes = sbuf("y_codes", [P, S], I32)
+        y_plane = sbuf("y_plane", [P, S], U8)
+        y_out = out_0.rearrange("(p t) c -> p t c", t=PACK)
+        for t, c0, c1 in pieces:
+            for i in range(4):
+                fetch(h_at[t][:, i, c0:c1], t, n_l[2 + i], c0, c1)
+                if i % 2 == 1:
+                    nc.vector.scalar_tensor_tensor(
+                        prod[t][:, i // 2, c0:c1], h_at[t][:, i - 1, c0:c1], 0.75, h_at[t][:, i, c0:c1], ALU.mult, ALU.mult
+                    )
+            nc.vector.tensor_tensor(y[:, t, c0:c1], prod[t][:, 0, c0:c1], prod[t][:, 1, c0:c1], ALU.subtract)
+            nc.sync.dma_start(y_out[:, t, c0:c1], y[:, t, c0:c1])
+            if t == PACK - 1:
+                round_and_quantise(y, y_bf, y_codes, y_plane, c0, c1)
+
+        nc.sync.dma_start(out_1[0].rearrange("p n r -> p (n r)").bitcast(I32), y_codes[:])
+        for q in range(4):
+            queue = nc.scalar if q > 0 else nc.sync
+            queue.dma_start(out_2[0, 4 * q : 4 * q + 4, :].bitcast(I32), y_plane[32 * q : 32 * q + 4, :].bitcast(I32))

@@ -19,6 +19,7 @@ ALU = mybir.AluOpType
 P = 128
 PACK = 4
 HALF = S // 2
+LAST = HALF
 
 
 def tile_picked_twpqjointbdet_none_po_kernel(
@@ -39,20 +40,18 @@ def tile_picked_twpqjointbdet_none_po_kernel(
             nc.sync.dma_start(tile[:], src)
             return tile
 
-        d_bytes = sbuf("d_bytes", [P, G], U8)
-        x_bytes = sbuf("x_bytes", [P, T], U8)
+        def placed(name, shape, dtype, offset):
+            return picks.tile(shape, dtype, name=name, align_bytes=64, offset=offset)
 
         def load_scale_rows(tile, scales):
             words = scales[0].bitcast(I32)
             nc.sync.dma_start(tile[:].bitcast(I32), words.unsqueeze(1).to_broadcast([16, 8, words.shape[1]]))
-
-        def placed(name, shape, dtype, offset):
-            return picks.tile(shape, dtype, name=name, align_bytes=64, offset=offset)
+            return tile
 
         k2_l = load_list("k2_l", k2)
-        load_scale_rows(d_bytes, d_scales)
+        d_bytes = load_scale_rows(sbuf("d_bytes", [P, G], U8), d_scales)
         two_l = load_list("two_l", two)
-        load_scale_rows(x_bytes, x_scales)
+        x_bytes = load_scale_rows(sbuf("x_bytes", [P, T], U8), x_scales)
         k1_l = load_list("k1_l", k1)
         offs_l = load_list("offs_l", offs)
         d_tab = sbuf("d_tab", [P, G], I32)
@@ -73,10 +72,14 @@ def tile_picked_twpqjointbdet_none_po_kernel(
             w_raw[:].bitcast(U16).rearrange("p (m t) -> p t m", t=PACK),
         )
 
-        widths = [2 * S, 2 * S, 2 * S, S]
-        rows = [sbuf("rows%d" % t, [P, widths[t]], F32) for t in range(PACK)]
-        for t in range(PACK - 1):
-            nc.vector.memset(rows[t][:, S:], 0.0)
+        def row_tiles(name, wide):
+            tiles = [sbuf("%s%d" % (name, t), [P, 2 * S if t < wide else S], F32) for t in range(PACK)]
+            for t in range(wide):
+                nc.vector.memset(tiles[t][:, S:], 0.0)
+            return tiles
+
+        b_rows = row_tiles("b_rows", 2)
+        h_rows = row_tiles("h_rows", 3)
 
         def deal_bytes(dst, src):
             nc.vector.tensor_copy(dst.rearrange("p (t m) -> p t m", t=PACK), src.rearrange("p (m t) -> p t m", t=PACK))
@@ -107,53 +110,56 @@ def tile_picked_twpqjointbdet_none_po_kernel(
             )
 
         plane_b = sbuf("plane_b", [P, H + S], U8)
-        coded_scales(placed("bytes_b", [P, H + S], U8, 8704), plane_b, k2_l, two_l)
+        coded_scales(placed("bytes_b", [P, H + S], U8, 4096), plane_b, k2_l, two_l)
         seat_rows(plane_b)
-        w_bytes = placed("w_bytes", [P, N], U8, 8704)
-        nc.gpsimd.memset(w_bytes[:].bitcast(I32), 0)
-        for q in range(4):
-            nc.sync.dma_start(w_bytes[32 * q : 32 * q + 4, :].bitcast(I32), w1_scales[0, 4 * q : 4 * q + 4, :].bitcast(I32))
-        d_b = sbuf("d_b", [P, H], I32)
-        x_b = sbuf("x_b", [P, S], I32)
-        coded_words(placed("d_picked_b", [P, H], I32, 6016), d_b, x_b, k2_l, two_l)
+        w_bytes = load_scale_rows(placed("w_bytes", [P, N], U8, 4096 + 64), w1_scales)
+        d_b = placed("d_b", [P, H], I32, 16384)
+        x_b = placed("x_b", [P, S], I32, 4096 - 960)
+        coded_words(placed("d_picked_b", [P, H], I32, 4096 + 704), d_b, x_b, k2_l, two_l)
         b_acc = [ps.tile([P, S], F32, name="b_acc%d" % t, tag="bank%d" % t) for t in range(PACK)]
         for t in range(PACK):
             coded_product(b_acc[t][:], t, d_b, x_b, plane_b)
+            if t < PACK - 1:
+                nc.scalar.copy(b_rows[t][:, :S], b_acc[t][:])
+            else:
+                nc.vector.tensor_copy(b_rows[t][:, :S], b_acc[t][:])
 
         n_l = [load_list("n%d_l" % (i + 1), src) for i, src in enumerate((n1, n2, n3, n4, n5, n6))]
-        plane_a = placed("plane_a", [P, H + S], U8, 7872)
-        coded_scales(placed("bytes_a", [P, H + S], U8, 6080), plane_a, k1_l, offs_l)
+        plane_a = placed("plane_a", [P, H + S], U8, 3136)
+        coded_scales(placed("bytes_a", [P, H + S], U8, 4864), plane_a, k1_l, offs_l)
         seat_rows(plane_a)
         d_a = sbuf("d_a", [P, H], I32)
-        x_a = placed("x_a", [P, S], I32, 6848)
-        coded_words(placed("d_picked_a", [P, H], I32, 4032), d_a, x_a, k1_l, offs_l)
-        w_plane = placed("w_plane", [P, N], U8, 6080)
+        x_a = placed("x_a", [P, S], I32, 16384 - 960)
+        coded_words(placed("d_picked_a", [P, H], I32, 16384 + 64), d_a, x_a, k1_l, offs_l)
+        w_plane = placed("w_plane", [P, N], U8, 4864)
         deal_bytes(w_plane[:], w_bytes[:])
+        seat_rows(w_plane)
         a_acc = [ps.tile([P, 2, S], F32, name="a_acc%d" % u) for u in range(2)]
         for t in range(PACK):
             coded_product(a_acc[t // 2][:, t % 2, :], t, d_a, x_a, plane_a)
 
-        def fetch(out, t, lst, c0, c1):
-            nc.scalar.activation(out, rows[t][:].indirect(lst[:, c0 // 16 : c1 // 16]), ACT.Copy)
+        def fetch(out, row_tile, lst, c0, c1):
+            nc.scalar.activation(out, row_tile[:].indirect(lst[:, c0 // 16 : c1 // 16]), ACT.Copy)
 
-        pieces = [(0, 0, S), (1, 0, S), (2, 0, S), (3, 0, HALF), (3, HALF, S)]
-
-        b_at = [sbuf("b_at%d" % i, [P, PACK, S], F32) for i in range(2)]
-        diff = sbuf("diff", [P, PACK, S], F32)
-        th = placed("th", [P, PACK, S], F32, 0)
+        at_whole = sbuf("at_whole", [P, 2, 2, S], F32)
+        at_first = sbuf("at_first", [P, 2, 2, HALF], F32)
+        at_second = sbuf("at_second", [P, 2, 2, HALF], F32)
+        diff = placed("diff", [P, PACK, S], F32, 16384 + 2048)
+        th = sbuf("th", [P, PACK, S], F32)
         z = sbuf("z", [P, PACK, S], F32)
         z_bf = sbuf("z_bf", [P, S, PACK], BF16)
         z_codes = sbuf("z_codes", [P, S], I32)
         z_plane = sbuf("z_plane", [P, S], U8)
-        h_first = ps.tile([P, PACK, HALF], F32, name="h_first")
-        h_lead = ps.tile([P, HALF], F32, name="h_lead")
-        h_rest = ps.tile([P, PACK - 1, HALF], F32, name="h_rest", tag="bank0")
+        h_lead = [ps.tile([P, HALF], F32, name="h_lead%d" % u) for u in range(2)]
+        h_rest = [ps.tile([P, S], F32, name="h_rest%d" % t, tag="bank%d" % t) for t in range(PACK - 1)]
 
-        def round_and_quantise(src, bf, codes, plane, c0, c1):
+        def weave(src, bf, c0, c1):
             nc.vector.tensor_copy(
                 bf[:, c0:c1, :].rearrange("p (c i) t -> p c t i", i=4),
                 src[:, :, c0:c1].rearrange("p t (c i) -> p c t i", i=4),
             )
+
+        def quantise(bf, codes, plane, c0, c1):
             nc.vector.quantize_mx(
                 out=codes[:, c0:c1].bitcast(FP8X4), scales=plane[:, c0:c1],
                 in_=bf[:, c0:c1, :].rearrange("p c t -> p (c t)"),
@@ -165,29 +171,47 @@ def tile_picked_twpqjointbdet_none_po_kernel(
                 rhs=z_codes[:, c0:c1].bitcast(FP8X4), rhs_scale=z_plane[:, c0:c1], start=True, stop=True,
             )
 
-        for t, c0, c1 in pieces:
-            if c0 == 0:
-                nc.scalar.copy(rows[t][:, :S], b_acc[t][:])
-            fetch(b_at[0][:, t, c0:c1], t, n_l[0], c0, c1)
-            fetch(b_at[1][:, t, c0:c1], t, n_l[1], c0, c1)
-            nc.vector.tensor_tensor(diff[:, t, c0:c1], b_at[0][:, t, c0:c1], b_at[1][:, t, c0:c1], ALU.subtract)
-            nc.scalar.activation(th[:, t, c0:c1], diff[:, t, c0:c1], ACT.Tanh, scale=0.0625)
-            nc.vector.scalar_tensor_tensor(
-                z[:, t, c0:c1], a_acc[t // 2][:, t % 2, c0:c1], gain[:, t : t + 1], th[:, t, c0:c1], ALU.mult, ALU.mult
-            )
-            if t == PACK - 1:
-                round_and_quantise(z, z_bf, z_codes, z_plane, c0, c1)
+        def fetch_b(dst, t, c0, c1):
+            for i in range(2):
+                fetch(dst[:, i, :], b_rows[t], n_l[i], c0, c1)
 
-        for t in range(PACK):
-            dense(h_first[:, t, :], t, 0, HALF)
-        dense(h_lead[:], 0, HALF, S)
+        def subtract(src, t0, t1, c0, c1):
+            nc.vector.tensor_tensor(diff[:, t0:t1, c0:c1], src[:, :, 0, :], src[:, :, 1, :], ALU.subtract)
+
+        def gate(t0, t1, c0, c1):
+            nc.scalar.activation(th[:, t0:t1, c0:c1], diff[:, t0:t1, c0:c1], ACT.Tanh, scale=0.0625)
+            for t in range(t0, t1):
+                nc.vector.scalar_tensor_tensor(
+                    z[:, t, c0:c1], a_acc[t // 2][:, t % 2, c0:c1], gain[:, t : t + 1], th[:, t, c0:c1], ALU.mult, ALU.mult
+                )
+
+        def close_half(u):
+            c0, c1 = HALF * u, HALF * (u + 1)
+            weave(z, z_bf, c0, c1)
+            quantise(z_bf, z_codes, z_plane, c0, c1)
+            dense(h_lead[u][:], 0, c0, c1)
+
+        for t in range(2):
+            fetch_b(at_whole[:, t], t, 0, S)
+        subtract(at_whole[:], 0, 2, 0, S)
+        for t in range(2, PACK):
+            fetch_b(at_first[:, t - 2], t, 0, HALF)
+        subtract(at_first[:], 2, PACK, 0, HALF)
+        gate(0, PACK, 0, HALF)
+        close_half(0)
+        fetch_b(at_second[:, 0], 2, HALF, S)
+        subtract(at_second[:, 0:1], 2, 3, HALF, S)
+        gate(0, 3, HALF, S)
+        fetch_b(at_second[:, 1], 3, HALF, S)
+        subtract(at_second[:, 1:2], 3, PACK, HALF, S)
+        gate(3, PACK, HALF, S)
+        close_half(1)
+        for u in range(2):
+            nc.scalar.copy(h_rows[0][:, HALF * u : HALF * (u + 1)], h_lead[u][:])
+
         for t in range(1, PACK):
-            dense(h_rest[:, t - 1, :], t, HALF, S)
-        for t in range(PACK):
-            nc.scalar.copy(rows[t][:, :HALF], h_first[:, t, :])
-        nc.scalar.copy(rows[0][:, HALF:S], h_lead[:])
-        for t in range(1, PACK):
-            nc.vector.tensor_copy(rows[t][:, HALF:S], h_rest[:, t - 1, :])
+            dense(h_rest[t - 1][:], t, 0, S)
+            nc.vector.tensor_copy(h_rows[t][:, :S], h_rest[t - 1][:])
 
         h_at = [sbuf("h_at%d" % t, [P, 4, S], F32) for t in range(PACK)]
         prod = [sbuf("prod%d" % t, [P, 2, S], F32) for t in range(PACK)]
@@ -195,20 +219,27 @@ def tile_picked_twpqjointbdet_none_po_kernel(
         y_bf = sbuf("y_bf", [P, S, PACK], BF16)
         y_codes = sbuf("y_codes", [P, S], I32)
         y_plane = sbuf("y_plane", [P, S], U8)
+        words_out = out_1[0].rearrange("p n r -> p (n r)").bitcast(I32)
         y_out = out_0.rearrange("(p t) c -> p t c", t=PACK)
-        for t, c0, c1 in pieces:
+        for t, c0, c1 in [(0, 0, S), (1, 0, S), (2, 0, S), (3, 0, HALF), (3, HALF, S)]:
             for i in range(4):
-                fetch(h_at[t][:, i, c0:c1], t, n_l[2 + i], c0, c1)
+                fetch(h_at[t][:, i, c0:c1], h_rows[t], n_l[2 + i], c0, c1)
                 if i % 2 == 1:
                     nc.vector.scalar_tensor_tensor(
                         prod[t][:, i // 2, c0:c1], h_at[t][:, i - 1, c0:c1], 0.75, h_at[t][:, i, c0:c1], ALU.mult, ALU.mult
                     )
             nc.vector.tensor_tensor(y[:, t, c0:c1], prod[t][:, 0, c0:c1], prod[t][:, 1, c0:c1], ALU.subtract)
-            nc.sync.dma_start(y_out[:, t, c0:c1], y[:, t, c0:c1])
+            if t < PACK - 1:
+                nc.sync.dma_start(y_out[:, t, :], y[:, t, :])
             if t == PACK - 1:
-                round_and_quantise(y, y_bf, y_codes, y_plane, c0, c1)
+                weave(y, y_bf, c0, c1)
+                quantise(y_bf, y_codes, y_plane, c0, c1)
+            if c1 == LAST:
+                nc.sync.dma_start(y_out[:, t, :LAST], y[:, t, :LAST])
+                nc.sync.dma_start(words_out[:, :LAST], y_codes[:, :LAST])
 
-        nc.sync.dma_start(out_1[0].rearrange("p n r -> p (n r)").bitcast(I32), y_codes[:])
+        nc.scalar.dma_start(y_out[:, PACK - 1, LAST:], y[:, PACK - 1, LAST:])
+        nc.sync.dma_start(words_out[:, LAST:], y_codes[:, LAST:])
         for q in range(4):
-            queue = nc.scalar if q > 0 else nc.sync
+            queue = nc.scalar if q > 1 else nc.sync
             queue.dma_start(out_2[0, 4 * q : 4 * q + 4, :].bitcast(I32), y_plane[32 * q : 32 * q + 4, :].bitcast(I32))

from contextlib import ExitStack

import concourse.mybir as mybir

K, T, S, N, G, H = 512, 1024, 256, 512, 2048, 512
FLOPS = 3 * 2 * 512 * 512 * 256

F32 = mybir.dt.float32
BF16 = mybir.dt.bfloat16
I32 = mybir.dt.int32
U32 = mybir.dt.uint32
U16 = mybir.dt.uint16
U8 = mybir.dt.uint8
FP8X4 = mybir.dt.float8_e4m3fn_x4
FP4X4 = mybir.dt.float4_e2m1fn_x4
ACT = mybir.ActivationFunctionType
ALU = mybir.AluOpType

P = 128
PACK = 4
HALF = S // 2
LAST = HALF


def tile_picked_twpqjointbdet_none_po_kernel(
    tc, x_words, x_scales, d_words, d_scales, gn, w1_words, w1_scales,
    offs, k1, two, k2, n1, n2, n3, n4, n5, n6, out_0, out_1, out_2,
):
    nc = tc.nc
    with ExitStack() as ctx:
        sb = ctx.enter_context(tc.tile_pool(name="sb", bufs=1))
        picks = ctx.enter_context(tc.tile_pool(name="picks", bufs=1))
        ps = ctx.enter_context(tc.psum_pool(name="ps", bufs=1))

        def sbuf(name, shape, dtype):
            return sb.tile(shape, dtype, name=name, align_bytes=64)

        def load_list(name, src):
            tile = sbuf(name, list(src.shape), U16)
            nc.sync.dma_start(tile[:], src)
            return tile

        def placed(name, shape, dtype, offset):
            return picks.tile(shape, dtype, name=name, align_bytes=64, offset=offset)

        def load_scale_rows(tile, scales):
            words = scales[0].bitcast(I32)
            nc.sync.dma_start(tile[:].bitcast(I32), words.unsqueeze(1).to_broadcast([16, 8, words.shape[1]]))
            return tile

        k2_l = load_list("k2_l", k2)
        d_bytes = load_scale_rows(sbuf("d_bytes", [P, G], U8), d_scales)
        two_l = load_list("two_l", two)
        x_bytes = load_scale_rows(sbuf("x_bytes", [P, T], U8), x_scales)
        k1_l = load_list("k1_l", k1)
        offs_l = load_list("offs_l", offs)
        d_tab = sbuf("d_tab", [P, G], I32)
        x_tab = sbuf("x_tab", [P, T], I32)
        nc.sync.dma_start(x_tab[:], x_words[0].rearrange("p n r -> p (n r)").bitcast(I32))
        nc.sync.dma_start(d_tab[:], d_words[0].rearrange("p n r -> p (n r)").bitcast(I32))

        gain_raw = sbuf("gain_raw", [P, PACK], F32)
        nc.gpsimd.dma_start(gain_raw[:], gn.rearrange("(p t) o -> p (t o)", t=PACK))
        w_raw = sbuf("w_raw", [P, 2 * N], U8)
        nc.gpsimd.dma_start(w_raw[:].bitcast(I32), w1_words[0].bitcast(I32))

        gain = sbuf("gain", [P, PACK], F32)
        nc.scalar.activation(gain[:], gain_raw[:], ACT.Copy, scale=0.0625)
        w_codes = sbuf("w_codes", [P, 2 * N], U8)
        nc.scalar.copy(
            w_codes[:].bitcast(U16).rearrange("p (t m) -> p t m", t=PACK),
            w_raw[:].bitcast(U16).rearrange("p (m t) -> p t m", t=PACK),
        )

        def row_tiles(name, wide):
            tiles = [sbuf("%s%d" % (name, t), [P, 2 * S if t < wide else S], F32) for t in range(PACK)]
            for t in range(wide):
                nc.vector.memset(tiles[t][:, S:], 0.0)
            return tiles

        b_rows = row_tiles("b_rows", 2)
        h_rows = row_tiles("h_rows", 3)

        def deal_bytes(dst, src):
            nc.vector.tensor_copy(dst.rearrange("p (t m) -> p t m", t=PACK), src.rearrange("p (m t) -> p t m", t=PACK))

        def coded_scales(picked, plane, k_l, x_l):
            nc.vector.tensor_copy(picked[:, :H], d_bytes[:].indirect(k_l[:]))
            nc.vector.tensor_copy(picked[:, H:], x_bytes[:].indirect(x_l[:]))
            deal_bytes(plane[:, :H], picked[:, :H])
            nc.vector.tensor_copy(plane[:, H : H + S].bitcast(I32), picked[:, H:].bitcast(I32))

        def seat_rows(plane):
            for r in range(1, 4):
                nc.sync.dma_start(plane[r:P:32, :].bitcast(I32), plane[8 * r : P : 32, :].bitcast(I32))

        def coded_words(d_picked, d_dealt, x_picked, k_l, x_l):
            nc.vector.tensor_copy(x_picked[:].bitcast(U32), x_tab[:].bitcast(U32).indirect(x_l[:]))
            nc.vector.tensor_copy(d_picked[:].bitcast(U32), d_tab[:].bitcast(U32).indirect(k_l[:]))
            nc.vector.tensor_copy(
                d_dealt[:].rearrange("p (t c i) -> p c t i", t=PACK, i=4),
                d_picked[:].rearrange("p (c i t) -> p c t i", t=PACK, i=4),
            )

        def coded_product(acc, t, d_dealt, x_picked, plane):
            cols = slice(P * t, P * (t + 1))
            nc.tensor.matmul_mx(
                acc, lhsT=d_dealt[:, cols].bitcast(FP8X4), lhsT_scale=plane[:, cols],
                rhs=x_picked[:].bitcast(FP8X4), rhs_scale=plane[:, H : H + S], start=True, stop=True,
            )

        plane_b = sbuf("plane_b", [P, H + S], U8)
        coded_scales(placed("bytes_b", [P, H + S], U8, 4096), plane_b, k2_l, two_l)
        seat_rows(plane_b)
        w_bytes = load_scale_rows(placed("w_bytes", [P, N], U8, 4096 + 64), w1_scales)
        d_b = placed("d_b", [P, H], I32, 16384)
        x_b = placed("x_b", [P, S], I32, 4096 - 960)
        coded_words(placed("d_picked_b", [P, H], I32, 4096 + 704), d_b, x_b, k2_l, two_l)
        b_acc = [ps.tile([P, S], F32, name="b_acc%d" % t, tag="bank%d" % t) for t in range(PACK)]
        for t in range(PACK):
            coded_product(b_acc[t][:], t, d_b, x_b, plane_b)
            if t < PACK - 1:
                nc.scalar.copy(b_rows[t][:, :S], b_acc[t][:])
            else:
                nc.vector.tensor_copy(b_rows[t][:, :S], b_acc[t][:])

        n_l = [load_list("n%d_l" % (i + 1), src) for i, src in enumerate((n1, n2, n3, n4, n5, n6))]
        plane_a = placed("plane_a", [P, H + S], U8, 3136)
        coded_scales(placed("bytes_a", [P, H + S], U8, 4864), plane_a, k1_l, offs_l)
        seat_rows(plane_a)
        d_a = sbuf("d_a", [P, H], I32)
        x_a = placed("x_a", [P, S], I32, 16384 - 960)
        coded_words(placed("d_picked_a", [P, H], I32, 16384 + 64), d_a, x_a, k1_l, offs_l)
        w_plane = placed("w_plane", [P, N], U8, 4864)
        deal_bytes(w_plane[:], w_bytes[:])
        seat_rows(w_plane)
        a_acc = [ps.tile([P, 2, S], F32, name="a_acc%d" % u) for u in range(2)]
        for t in range(PACK):
            coded_product(a_acc[t // 2][:, t % 2, :], t, d_a, x_a, plane_a)

        def fetch(out, row_tile, lst, c0, c1):
            nc.scalar.activation(out, row_tile[:].indirect(lst[:, c0 // 16 : c1 // 16]), ACT.Copy)

        at_whole = sbuf("at_whole", [P, 2, 2, S], F32)
        at_first = sbuf("at_first", [P, 2, 2, HALF], F32)
        at_second = sbuf("at_second", [P, 2, 2, HALF], F32)
        diff = placed("diff", [P, PACK, S], F32, 16384 + 2048)
        th = sbuf("th", [P, PACK, S], F32)
        z = sbuf("z", [P, PACK, S], F32)
        z_bf = sbuf("z_bf", [P, S, PACK], BF16)
        z_codes = sbuf("z_codes", [P, S], I32)
        z_plane = sbuf("z_plane", [P, S], U8)
        h_lead = [ps.tile([P, HALF], F32, name="h_lead%d" % u) for u in range(2)]
        h_rest = [ps.tile([P, S], F32, name="h_rest%d" % t, tag="bank%d" % t) for t in range(PACK - 1)]

        def weave(src, bf, c0, c1):
            nc.vector.tensor_copy(
                bf[:, c0:c1, :].rearrange("p (c i) t -> p c t i", i=4),
                src[:, :, c0:c1].rearrange("p t (c i) -> p c t i", i=4),
            )

        def quantise(bf, codes, plane, c0, c1):
            nc.vector.quantize_mx(
                out=codes[:, c0:c1].bitcast(FP8X4), scales=plane[:, c0:c1],
                in_=bf[:, c0:c1, :].rearrange("p c t -> p (c t)"),
            )

        def dense(acc, t, c0, c1):
            nc.tensor.matmul_mx(
                acc, lhsT=w_codes[:, 2 * P * t : 2 * P * (t + 1)].bitcast(FP4X4), lhsT_scale=w_plane[:, P * t : P * (t + 1)],
                rhs=z_codes[:, c0:c1].bitcast(FP8X4), rhs_scale=z_plane[:, c0:c1], start=True, stop=True,
            )

        def fetch_b(dst, t, c0, c1):
            for i in range(2):
                fetch(dst[:, i, :], b_rows[t], n_l[i], c0, c1)

        def subtract(src, t0, t1, c0, c1):
            nc.vector.tensor_tensor(diff[:, t0:t1, c0:c1], src[:, :, 0, :], src[:, :, 1, :], ALU.subtract)

        def gate(t0, t1, c0, c1):
            nc.scalar.activation(th[:, t0:t1, c0:c1], diff[:, t0:t1, c0:c1], ACT.Tanh, scale=0.0625)
            for t in range(t0, t1):
                nc.vector.scalar_tensor_tensor(
                    z[:, t, c0:c1], a_acc[t // 2][:, t % 2, c0:c1], gain[:, t : t + 1], th[:, t, c0:c1], ALU.mult, ALU.mult
                )

        def close_half(u):
            c0, c1 = HALF * u, HALF * (u + 1)
            weave(z, z_bf, c0, c1)
            quantise(z_bf, z_codes, z_plane, c0, c1)
            dense(h_lead[u][:], 0, c0, c1)

        for t in range(2):
            fetch_b(at_whole[:, t], t, 0, S)
        subtract(at_whole[:], 0, 2, 0, S)
        for t in range(2, PACK):
            fetch_b(at_first[:, t - 2], t, 0, HALF)
        subtract(at_first[:], 2, PACK, 0, HALF)
        gate(0, PACK, 0, HALF)
        close_half(0)
        fetch_b(at_second[:, 0], 2, HALF, S)
        subtract(at_second[:, 0:1], 2, 3, HALF, S)
        gate(0, 3, HALF, S)
        fetch_b(at_second[:, 1], 3, HALF, S)
        subtract(at_second[:, 1:2], 3, PACK, HALF, S)
        gate(3, PACK, HALF, S)
        close_half(1)
        for u in range(2):
            nc.scalar.copy(h_rows[0][:, HALF * u : HALF * (u + 1)], h_lead[u][:])

        for t in range(1, PACK):
            dense(h_rest[t - 1][:], t, 0, S)
            nc.vector.tensor_copy(h_rows[t][:, :S], h_rest[t - 1][:])

        h_at = [sbuf("h_at%d" % t, [P, 4, S], F32) for t in range(PACK)]
        prod = [sbuf("prod%d" % t, [P, 2, S], F32) for t in range(PACK)]
        y = sbuf("y", [P, PACK, S], F32)
        y_bf = sbuf("y_bf", [P, S, PACK], BF16)
        y_codes = sbuf("y_codes", [P, S], I32)
        y_plane = sbuf("y_plane", [P, S], U8)
        words_out = out_1[0].rearrange("p n r -> p (n r)").bitcast(I32)
        y_out = out_0.rearrange("(p t) c -> p t c", t=PACK)
        for t, c0, c1 in [(0, 0, S), (1, 0, S), (2, 0, S), (3, 0, HALF), (3, HALF, S)]:
            for i in range(4):
                fetch(h_at[t][:, i, c0:c1], h_rows[t], n_l[2 + i], c0, c1)
                if i % 2 == 1:
                    nc.vector.scalar_tensor_tensor(
                        prod[t][:, i // 2, c0:c1], h_at[t][:, i - 1, c0:c1], 0.75, h_at[t][:, i, c0:c1], ALU.mult, ALU.mult
                    )
            nc.vector.tensor_tensor(y[:, t, c0:c1], prod[t][:, 0, c0:c1], prod[t][:, 1, c0:c1], ALU.subtract)
            if t < PACK - 1:
                nc.sync.dma_start(y_out[:, t, :], y[:, t, :])
            if t == PACK - 1:
                weave(y, y_bf, c0, c1)
                quantise(y_bf, y_codes, y_plane, c0, c1)
            if c1 == LAST:
                nc.sync.dma_start(y_out[:, t, :LAST], y[:, t, :LAST])
                nc.sync.dma_start(words_out[:, :LAST], y_codes[:, :LAST])

        nc.scalar.dma_start(y_out[:, PACK - 1, LAST:], y[:, PACK - 1, LAST:])
        nc.sync.dma_start(words_out[:, LAST:], y_codes[:, LAST:])
        for q in range(4):
            queue = nc.scalar if q > 1 else nc.sync
            queue.dma_start(out_2[0, 4 * q : 4 * q + 4, :].bitcast(I32), y_plane[32 * q : 32 * q + 4, :].bitcast(I32))
